import numpy as np
import ml_dtypes

BF16 = ml_dtypes.bfloat16


def bf(x):
    return np.asarray(x, np.float32).astype(BF16)


def f32(x):
    return np.asarray(x, np.float32)


def f64(x):
    return np.asarray(x).astype(np.float64)


def striped(idx):
    return np.concatenate([l.reshape(-1, 16).T for l in idx])


def rows(idx, k):
    return np.tile(np.repeat(idx, 16, axis=0), (k // (16 * 8), 1))


def look(tab, idx):
    return np.take_along_axis(f64(tab), rows(idx, len(tab)), axis=1)


K, S, V, N, M = 128, 2048, 1024, 1024, 128


def silu(v):
    return v / (1.0 + np.exp(-v))


def setup_inputs():
    return {"tab": f32(np.random.standard_normal((2, K, S))), "y": f32(np.random.standard_normal((K, V))), "w": bf(np.random.standard_normal((K, M)) / np.sqrt(K)), "b": f32(0.5 * np.random.standard_normal((M, 1))), "offs": striped(np.stack([np.random.permutation(S)[:N] for _ in range(8)]))}


def reference(tab, y, w, b, offs):
    idx = np.stack([g.T.reshape(-1) for g in np.split(offs, 8)])
    x = (look(tab[0], idx) - f64(y)) * (silu(look(tab[1], idx)))
    return np.maximum(f64(w).T @ x + f64(b), 0.0)

@@ -1,0 +1,45 @@
+import concourse.mybir as mybir
+
+F32, BF16, U16 = mybir.dt.float32, mybir.dt.bfloat16, mybir.dt.uint16
+ALU = mybir.AluOpType
+ACT = mybir.ActivationFunctionType
+
+K, S, N, M = 128, 2048, 1024, 128
+PIECE = 512
+FLOPS = 2 * K * M * N
+
+
+def tile_lookup_vg_subsilu_relu_kernel(tc, tab, y, w, b, offs, out):
+    nc = tc.nc
+    with (
+        tc.tile_pool(name="held", bufs=1) as held,
+        tc.tile_pool(name="work", bufs=2) as work,
+        tc.psum_pool(name="psum", bufs=2) as psum,
+    ):
+        offsets = held.tile([K, N // 16], U16)
+        values = held.tile([K, S], F32)
+        gates = held.tile([K, S], F32)
+        stream = held.tile([K, N], F32)
+        weights = held.tile([K, M], BF16)
+        bias = held.tile([M, 1], F32)
+        nc.sync.dma_start(offsets[:], offs)
+        nc.sync.dma_start(values[:], tab[0])
+        nc.sync.dma_start(gates[:], tab[1])
+        nc.sync.dma_start(stream[:], y)
+        nc.sync.dma_start(weights[:], w)
+        nc.sync.dma_start(bias[:], b)
+
+        for p in range(N // PIECE):
+            cols = slice(p * PIECE, (p + 1) * PIECE)
+            picks = offsets[:, p * PIECE // 16 : (p + 1) * PIECE // 16]
+            diff = work.tile([K, PIECE], F32)
+            gate = work.tile([K, PIECE], F32)
+            x = work.tile([K, PIECE], BF16)
+            acc = psum.tile([M, PIECE], F32)
+            res = work.tile([M, PIECE], F32)
+            nc.vector.tensor_tensor(diff[:], values[:].indirect(picks), stream[:, cols], ALU.subtract)
+            nc.scalar.activation(gate[:], gates[:].indirect(picks), ACT.Silu)
+            nc.vector.tensor_tensor(x[:], diff[:], gate[:], ALU.mult)
+            nc.tensor.matmul(acc[:], weights[:], x[:], start=True, stop=True)
+            nc.scalar.activation(res[:], acc[:], ACT.Relu, bias=bias[:])
+            nc.sync.dma_start(out[:, cols], res[:])

@@ -6,6 +6,7 @@ ACT = mybir.ActivationFunctionType
 
 K, S, N, M = 128, 2048, 1024, 128
 PIECE = 512
+CHUNK = 256
 FLOPS = 2 * K * M * N
 
 
@@ -13,8 +14,8 @@ def tile_lookup_vg_subsilu_relu_kernel(tc, tab, y, w, b, offs, out):
     nc = tc.nc
     with (
         tc.tile_pool(name="held", bufs=1) as held,
-        tc.tile_pool(name="work", bufs=2) as work,
-        tc.psum_pool(name="psum", bufs=2) as psum,
+        tc.tile_pool(name="work", bufs=N // CHUNK) as work,
+        tc.psum_pool(name="psum", bufs=N // CHUNK) as psum,
     ):
         offsets = held.tile([K, N // 16], U16)
         values = held.tile([K, S], F32)
@@ -22,24 +23,34 @@ def tile_lookup_vg_subsilu_relu_kernel(tc, tab, y, w, b, offs, out):
         stream = held.tile([K, N], F32)
         weights = held.tile([K, M], BF16)
         bias = held.tile([M, 1], F32)
+        diff = held.tile([K, N], F32)
+        gate = held.tile([K, N], F32)
+
         nc.sync.dma_start(offsets[:], offs)
         nc.sync.dma_start(values[:], tab[0])
+        nc.sync.dma_start(stream[:, :PIECE], y[:, :PIECE])
         nc.sync.dma_start(gates[:], tab[1])
-        nc.sync.dma_start(stream[:], y)
+        nc.sync.dma_start(stream[:, PIECE:], y[:, PIECE:])
         nc.sync.dma_start(weights[:], w)
         nc.sync.dma_start(bias[:], b)
+
+        warm = held.tile([K, 8], F32)
+        warm_out = held.tile([K, 8], F32)
+        nc.vector.memset(warm[:], 0.0)
+        nc.scalar.activation(warm_out[:], warm[:], ACT.Silu)
 
         for p in range(N // PIECE):
             cols = slice(p * PIECE, (p + 1) * PIECE)
             picks = offsets[:, p * PIECE // 16 : (p + 1) * PIECE // 16]
-            diff = work.tile([K, PIECE], F32)
-            gate = work.tile([K, PIECE], F32)
-            x = work.tile([K, PIECE], BF16)
-            acc = psum.tile([M, PIECE], F32)
-            res = work.tile([M, PIECE], F32)
-            nc.vector.tensor_tensor(diff[:], values[:].indirect(picks), stream[:, cols], ALU.subtract)
-            nc.scalar.activation(gate[:], gates[:].indirect(picks), ACT.Silu)
-            nc.vector.tensor_tensor(x[:], diff[:], gate[:], ALU.mult)
+            nc.vector.tensor_tensor(diff[:, cols], values[:].indirect(picks), stream[:, cols], ALU.subtract)
+            nc.scalar.activation(gate[:, cols], gates[:].indirect(picks), ACT.Silu)
+
+        for c in range(N // CHUNK):
+            cols = slice(c * CHUNK, (c + 1) * CHUNK)
+            x = work.tile([K, CHUNK], BF16)
+            acc = psum.tile([M, CHUNK], F32)
+            res = work.tile([M, CHUNK], F32)
+            nc.vector.tensor_tensor(x[:], diff[:, cols], gate[:, cols], ALU.mult)
             nc.tensor.matmul(acc[:], weights[:], x[:], start=True, stop=True)
             nc.scalar.activation(res[:], acc[:], ACT.Relu, bias=bias[:])
             nc.sync.dma_start(out[:, cols], res[:])

@@ -6,7 +6,8 @@ ACT = mybir.ActivationFunctionType
 
 K, S, N, M = 128, 2048, 1024, 128
 PIECE = 512
-CHUNK = 256
+CHUNK = 128
+STORE = 256
 FLOPS = 2 * K * M * N
 
 
@@ -25,9 +26,10 @@ def tile_lookup_vg_subsilu_relu_kernel(tc, tab, y, w, b, offs, out):
         bias = held.tile([M, 1], F32)
         diff = held.tile([K, N], F32)
         gate = held.tile([K, N], F32)
+        res = held.tile([M, N], F32)
 
-        nc.sync.dma_start(offsets[:], offs)
         nc.sync.dma_start(values[:], tab[0])
+        nc.sync.dma_start(offsets[:], offs)
         nc.sync.dma_start(stream[:, :PIECE], y[:, :PIECE])
         nc.sync.dma_start(gates[:], tab[1])
         nc.sync.dma_start(stream[:, PIECE:], y[:, PIECE:])
@@ -49,8 +51,12 @@ def tile_lookup_vg_subsilu_relu_kernel(tc, tab, y, w, b, offs, out):
             cols = slice(c * CHUNK, (c + 1) * CHUNK)
             x = work.tile([K, CHUNK], BF16)
             acc = psum.tile([M, CHUNK], F32)
-            res = work.tile([M, CHUNK], F32)
             nc.vector.tensor_tensor(x[:], diff[:, cols], gate[:, cols], ALU.mult)
             nc.tensor.matmul(acc[:], weights[:], x[:], start=True, stop=True)
-            nc.scalar.activation(res[:], acc[:], ACT.Relu, bias=bias[:])
-            nc.sync.dma_start(out[:, cols], res[:])
+            if cols.stop <= N - STORE:
+                nc.scalar.activation(res[:, cols], acc[:], ACT.Relu, bias=bias[:])
+            else:
+                nc.vector.tensor_scalar(res[:, cols], acc[:], bias[:], 0.0, ALU.add, ALU.max)
+            if cols.stop % STORE == 0:
+                done = slice(cols.stop - STORE, cols.stop)
+                nc.sync.dma_start(out[:, done], res[:, done])

@@ -7,7 +7,6 @@ ACT = mybir.ActivationFunctionType
 K, S, N, M = 128, 2048, 1024, 128
 PIECE = 512
 CHUNK = 128
-STORE = 256
 FLOPS = 2 * K * M * N
 
 
@@ -47,16 +46,17 @@ def tile_lookup_vg_subsilu_relu_kernel(tc, tab, y, w, b, offs, out):
             nc.vector.tensor_tensor(diff[:, cols], values[:].indirect(picks), stream[:, cols], ALU.subtract)
             nc.scalar.activation(gate[:, cols], gates[:].indirect(picks), ACT.Silu)
 
+        idle = psum.tile([M, PIECE], F32, tag="acc")
+        nc.tensor.matmul(idle[:], diff[:, :M], diff[:, :PIECE], start=True, stop=True)
+
         for c in range(N // CHUNK):
             cols = slice(c * CHUNK, (c + 1) * CHUNK)
             x = work.tile([K, CHUNK], BF16)
             acc = psum.tile([M, CHUNK], F32)
             nc.vector.tensor_tensor(x[:], diff[:, cols], gate[:, cols], ALU.mult)
             nc.tensor.matmul(acc[:], weights[:], x[:], start=True, stop=True)
-            if cols.stop <= N - STORE:
+            if c < N // CHUNK - 2:
                 nc.scalar.activation(res[:, cols], acc[:], ACT.Relu, bias=bias[:])
             else:
                 nc.vector.tensor_scalar(res[:, cols], acc[:], bias[:], 0.0, ALU.add, ALU.max)
-            if cols.stop % STORE == 0:
-                done = slice(cols.stop - STORE, cols.stop)
-                nc.sync.dma_start(out[:, done], res[:, done])
+            nc.sync.dma_start(out[:, cols], res[:, cols])

@@ -27,13 +27,13 @@ def tile_lookup_vg_subsilu_relu_kernel(tc, tab, y, w, b, offs, out):
         gate = held.tile([K, N], F32)
         res = held.tile([M, N], F32)
 
-        nc.sync.dma_start(values[:], tab[0])
         nc.sync.dma_start(offsets[:], offs)
-        nc.sync.dma_start(stream[:, :PIECE], y[:, :PIECE])
+        nc.sync.dma_start(values[:], tab[0])
         nc.sync.dma_start(gates[:], tab[1])
         nc.sync.dma_start(stream[:, PIECE:], y[:, PIECE:])
-        nc.sync.dma_start(weights[:], w)
-        nc.sync.dma_start(bias[:], b)
+        nc.scalar.dma_start(stream[:, :PIECE], y[:, :PIECE])
+        nc.scalar.dma_start(weights[:], w)
+        nc.scalar.dma_start(bias[:], b)
 
         warm = held.tile([K, 8], F32)
         warm_out = held.tile([K, 8], F32)
@@ -45,9 +45,6 @@ def tile_lookup_vg_subsilu_relu_kernel(tc, tab, y, w, b, offs, out):
             picks = offsets[:, p * PIECE // 16 : (p + 1) * PIECE // 16]
             nc.vector.tensor_tensor(diff[:, cols], values[:].indirect(picks), stream[:, cols], ALU.subtract)
             nc.scalar.activation(gate[:, cols], gates[:].indirect(picks), ACT.Silu)
-
-        idle = psum.tile([M, PIECE], F32, tag="acc")
-        nc.tensor.matmul(idle[:], diff[:, :M], diff[:, :PIECE], start=True, stop=True)
 
         for c in range(N // CHUNK):
             cols = slice(c * CHUNK, (c + 1) * CHUNK)

import concourse.mybir as mybir

F32, BF16, U16 = mybir.dt.float32, mybir.dt.bfloat16, mybir.dt.uint16
ALU = mybir.AluOpType
ACT = mybir.ActivationFunctionType

K, S, N, M = 128, 2048, 1024, 128
PIECE = 512
CHUNK = 128
FLOPS = 2 * K * M * N


def tile_lookup_vg_subsilu_relu_kernel(tc, tab, y, w, b, offs, out):
    nc = tc.nc
    with (
        tc.tile_pool(name="held", bufs=1) as held,
        tc.tile_pool(name="work", bufs=N // CHUNK) as work,
        tc.psum_pool(name="psum", bufs=N // CHUNK) as psum,
    ):
        offsets = held.tile([K, N // 16], U16)
        values = held.tile([K, S], F32)
        gates = held.tile([K, S], F32)
        stream = held.tile([K, N], F32)
        weights = held.tile([K, M], BF16)
        bias = held.tile([M, 1], F32)
        diff = held.tile([K, N], F32)
        gate = held.tile([K, N], F32)
        res = held.tile([M, N], F32)

        nc.sync.dma_start(offsets[:], offs)
        nc.sync.dma_start(values[:], tab[0])
        nc.sync.dma_start(gates[:], tab[1])
        nc.sync.dma_start(stream[:, PIECE:], y[:, PIECE:])
        nc.scalar.dma_start(stream[:, :PIECE], y[:, :PIECE])
        nc.scalar.dma_start(weights[:], w)
        nc.scalar.dma_start(bias[:], b)

        warm = held.tile([K, 8], F32)
        warm_out = held.tile([K, 8], F32)
        nc.vector.memset(warm[:], 0.0)
        nc.scalar.activation(warm_out[:], warm[:], ACT.Silu)

        for p in range(N // PIECE):
            cols = slice(p * PIECE, (p + 1) * PIECE)
            picks = offsets[:, p * PIECE // 16 : (p + 1) * PIECE // 16]
            nc.vector.tensor_tensor(diff[:, cols], values[:].indirect(picks), stream[:, cols], ALU.subtract)
            nc.scalar.activation(gate[:, cols], gates[:].indirect(picks), ACT.Silu)

        for c in range(N // CHUNK):
            cols = slice(c * CHUNK, (c + 1) * CHUNK)
            x = work.tile([K, CHUNK], BF16)
            acc = psum.tile([M, CHUNK], F32)
            nc.vector.tensor_tensor(x[:], diff[:, cols], gate[:, cols], ALU.mult)
            nc.tensor.matmul(acc[:], weights[:], x[:], start=True, stop=True)
            if c < N // CHUNK - 2:
                nc.scalar.activation(res[:, cols], acc[:], ACT.Relu, bias=bias[:])
            else:
                nc.vector.tensor_scalar(res[:, cols], acc[:], bias[:], 0.0, ALU.add, ALU.max)
            nc.sync.dma_start(out[:, cols], res[:, cols])
